import numpy as np
import ml_dtypes


def mxq(x, axis, fmt="e4m3"):
    dtype, down = {"e4m3": (ml_dtypes.float8_e4m3fn, 7), "e5m2": (ml_dtypes.float8_e5m2, 14)}[fmt]
    v = np.moveaxis(np.asarray(x, np.float32).astype(ml_dtypes.bfloat16).astype(np.float64), axis, -1)
    blocks = v.reshape(v.shape[:-1] + (-1, 32))
    amax = np.abs(blocks).max(-1, keepdims=True)
    byte = np.maximum(np.where(amax > 0, np.frexp(amax)[1] - 1 + 127, 0) - down, 1)
    scale = np.exp2(byte - 127.0)
    codes = (blocks / scale).astype(np.float32).astype(dtype).astype(np.float64)
    return np.moveaxis((codes * scale).reshape(v.shape), -1, axis)


WIDE = False


def mx_kscale(k):
    if not WIDE:
        return np.ones(k)
    levels = np.array([10, -10, 5, -5, 0])
    if k % 512:
        return np.exp2(np.random.permutation(np.resize(levels, k // 32))).repeat(32)
    a = np.empty((k // 512, 16))
    for p in range(k // 512):
        a[p, :8] = np.random.permutation(np.resize(levels, 8))
        for g in range(8):
            far = levels[np.abs(levels - a[p, g]) >= 10]
            a[p, g + 8] = far[np.random.randint(len(far))]
    return np.exp2(a.ravel()).repeat(32)


def f64(x):
    return np.asarray(x).astype(np.float64)


def striped(idx):
    return np.tile(idx.reshape(-1, 16).T, (8, 1)).astype(np.uint16)


def unstriped(offs):
    return offs[:16].T.reshape(-1).astype(np.int64)


E2M1 = np.array([0.0, 0.5, 1.0, 1.5, 2.0, 3.0, 4.0, 6.0, -0.0, -0.5, -1.0, -1.5, -2.0, -3.0, -4.0, -6.0])


def pack_weight(w, fmt):
    k, n = w.shape
    w = f64(np.asarray(w, np.float32).astype(ml_dtypes.bfloat16)).reshape(k // 32, 32, n)
    amax = np.abs(w).max(1)
    if fmt == "e4m3":
        byte = np.frexp(amax)[1] - 1 + 127 - 7
    else:
        mant, ex = np.frexp(amax / 6.0)
        byte = np.where(mant > 0.5, ex, ex - 1) + 127
    byte = np.clip(np.where(amax > 0, byte, 1), 1, 254)
    scaled = (w * np.exp2(127.0 - byte)[:, None, :]).reshape(k, n).astype(np.float32)
    by_word = np.ascontiguousarray(scaled.reshape(k // 512, 128, 4, n).transpose(0, 1, 3, 2))
    if fmt == "e4m3":
        words = by_word.astype(ml_dtypes.float8_e4m3fn).view(np.uint8)
    else:
        c = by_word.astype(ml_dtypes.float4_e2m1fn).view(np.uint8) & 0xF
        words = (c[..., 0::2] | (c[..., 1::2] << 4)).reshape(k // 512, 128, 2 * n)
    return np.ascontiguousarray(words), np.ascontiguousarray(byte.astype(np.uint8).reshape(k // 512, 16, n))


def unpack_weight(words, scales, fmt):
    g, _, n = scales.shape
    words = np.ascontiguousarray(words).reshape(g, 128, n, -1)
    if fmt == "e4m3":
        vals = words.view(ml_dtypes.float8_e4m3fn).astype(np.float64)
    else:
        nib = np.empty((g, 128, n, 4), np.uint8)
        nib[..., 0::2] = words & 0xF
        nib[..., 1::2] = words >> 4
        vals = E2M1[nib]
    vals = vals * np.repeat(np.exp2(scales.astype(np.float64) - 127.0), 8, axis=1)[..., None]
    return vals.transpose(0, 1, 3, 2).reshape(g * 512, n)


def gelu(v):
    return 0.5 * v * (1.0 + np.tanh(np.sqrt(2.0 / np.pi) * (v + 0.044715 * v**3)))


K, K2, H, N, T, S = 1024, 512, 1024, 256, 2048, 1024

def setup_inputs():
    n = np.random.standard_normal
    s = mx_kscale(K)[:, None]
    s2 = mx_kscale(K2)[:, None]
    u = mx_kscale(H)[:, None]
    tab_words, tab_scales = pack_weight(n((K, T)) * s, "e4m3")
    tab2_words, tab2_scales = pack_weight(n((K2, T)) * s2, "e4m3")
    tab3_words, tab3_scales = pack_weight(n((K2, T)) * s2, "e2m1")
    w1_words, w1_scales = pack_weight(n((K, H)) / np.sqrt(K) / s * u.T, "e2m1")
    w3_words, w3_scales = pack_weight(0.45 * n((K2, H)) / np.sqrt(K2) / s2, "e4m3")
    return {
        "tab_words": tab_words, "tab_scales": tab_scales,
        "tab2_words": tab2_words, "tab2_scales": tab2_scales,
        "tab3_words": tab3_words, "tab3_scales": tab3_scales,
        "offs": striped(np.random.permutation(T)[:S]),
        "offs2": striped(np.random.permutation(T)[:S]),
        "offs3": striped(np.random.permutation(T)[:S]),
        "w1_words": w1_words, "w1_scales": w1_scales,
        "w2": (n((K2, H)) / np.sqrt(K2) / s2 * u.T).astype(np.float32),
        "w3_words": w3_words, "w3_scales": w3_scales,
        "w4": (n((H, N)) / np.sqrt(H) / u).astype(np.float32),
    }

def reference(tab_words, tab_scales, tab2_words, tab2_scales, tab3_words, tab3_scales, offs, offs2, offs3, w1_words, w1_scales, w2, w3_words, w3_scales, w4):
    v = unpack_weight(tab_words, tab_scales, "e4m3")[:, unstriped(offs)]
    v2 = unpack_weight(tab2_words, tab2_scales, "e4m3")[:, unstriped(offs2)]
    v3 = unpack_weight(tab3_words, tab3_scales, "e2m1")[:, unstriped(offs3)]
    w1 = unpack_weight(w1_words, w1_scales, "e2m1")
    w3 = unpack_weight(w3_words, w3_scales, "e4m3")
    x = w1.T @ v
    b = mxq(f64(w2), 0, "e4m3").T @ v2
    d = w3.T @ v3
    h = x * np.cos(d) + b * np.sin(d)
    return mxq(f64(w4), 0, "e4m3").T @ mxq(h, 0, "e4m3")

@@ -1,0 +1,274 @@
+import math
+from contextlib import ExitStack
+
+import concourse.mybir as mybir
+
+K, K2, H, N, T, S = 1024, 512, 1024, 256, 2048, 1024
+FLOPS = 2 * S * (K * H + 2 * K2 * H + H * N)
+
+F32 = mybir.dt.float32
+BF16 = mybir.dt.bfloat16
+I32 = mybir.dt.int32
+U32 = mybir.dt.uint32
+U16 = mybir.dt.uint16
+U8 = mybir.dt.uint8
+FP8X4 = mybir.dt.float8_e4m3fn_x4
+FP4X4 = mybir.dt.float4_e2m1fn_x4
+ACT = mybir.ActivationFunctionType
+ALU = mybir.AluOpType
+
+P = 128
+CHUNK = 256
+CHUNKS = S // CHUNK
+LEAD = 8
+EARLY = 6
+STAGE = (11, 15, 14, 13)
+VECTOR_SUMS = (15,)
+
+
+def tile_list_seasonal_plant_picks_kernel(
+    tc, tab_words, tab_scales, tab2_words, tab2_scales, tab3_words, tab3_scales,
+    offs, offs2, offs3, w1_words, w1_scales, w2, w3_words, w3_scales, w4, out,
+):
+    nc = tc.nc
+    with ExitStack() as ctx:
+        keep = ctx.enter_context(tc.tile_pool(name="keep", bufs=1))
+        ring = ctx.enter_context(tc.tile_pool(name="ring", bufs=2))
+        psum = ctx.enter_context(tc.psum_pool(name="psum", bufs=2))
+
+        def held(name, columns, dtype):
+            return keep.tile([P, columns], dtype, name=name, align_bytes=64)
+
+        list1 = keep.tile([P, S // 16], U16, name="list1")
+        list2 = keep.tile([P, S // 16], U16, name="list2")
+        list3 = keep.tile([P, S // 16], U16, name="list3")
+
+        day_words = held("day_words", T, U16)
+        day_scales = held("day_scales", T, U8)
+        shop_words = [held("shop_words%d" % a, T, U32) for a in range(2)]
+        shop_scales = held("shop_scales", T, U8)
+        plant_words = held("plant_words", T, U32)
+        plant_scales = held("plant_scales", T, U8)
+
+        v3_words = [held("v3_words", CHUNK, U16)]
+        v3_scales = held("v3_scales", S, U8)
+        v_words = [held("v_words%d" % a, S, U32) for a in range(2)]
+        v_scales = [held("v_scales%d" % a, S, U8) for a in range(2)]
+        v2_words = held("v2_words", S, U32)
+        v2_scales = held("v2_scales", S, U8)
+
+        w3_raw_words = held("w3_raw_words", H, I32)
+        w3_raw_scales = held("w3_raw_scales", H, U8)
+        w1_raw_words = held("w1_raw_words", H, I32)
+        w1_raw_scales = held("w1_raw_scales", 2 * H, U8)
+        w2_raw = held("w2_raw", 4 * H, F32)
+        w4_raw = [held("w4_raw%d" % g, 4 * N, F32) for g in range(2)]
+
+        w3_q = held("w3_q", H, U32)
+        w3_s = held("w3_s", H, U8)
+        w1_q = held("w1_q", 2 * H, U16)
+        w1_s = held("w1_s", 2 * H, U8)
+        w2_b = [held("w2_b%d" % g, 2 * H, BF16) for g in range(2)]
+        w2_q = held("w2_q", H, U32)
+        w2_s = held("w2_s", H, U8)
+        w4_q = held("w4_q", 2 * N, U32)
+        w4_s = held("w4_s", 2 * N, U8)
+
+        nc.vector.memset(shop_scales[:].bitcast(I32), 0)
+        nc.gpsimd.memset(v_scales[1][:].bitcast(I32), 0)
+        nc.vector.memset(plant_scales[:].bitcast(I32), 0)
+        nc.gpsimd.memset(w1_raw_scales[:].bitcast(I32), 0)
+
+        def load_scale_rows(tile, rows, quadrants=range(4)):
+            for q in quadrants:
+                nc.sync.dma_start(tile[32 * q : 32 * q + 4, :].bitcast(I32), rows[4 * q : 4 * q + 4, :].bitcast(I32))
+
+        def fill_scale_rows(tile, rows, quadrants):
+            for q in quadrants:
+                four = rows[4 * q : 4 * q + 4, :].bitcast(I32)
+                nc.sync.dma_start(tile[32 * q : 32 * q + 32, :].bitcast(I32), four.unsqueeze(0).broadcast_to([8, 4, four.shape[1]]))
+
+        def words_of(ap):
+            return ap.rearrange("p n t -> p (n t)").bitcast(I32)
+
+        def reorder(dst, src, run, g, passes):
+            d = dst[:].bitcast(I32).rearrange("p (a g t q i) -> p g a t q i", a=passes, g=2, t=4, i=run)
+            s = src[:].bitcast(I32).rearrange("p (a q g t i) -> p g a t q i", a=passes, g=2, t=4, i=run)
+            nc.vector.tensor_copy(d[:, g], s[:, g])
+
+        def gather(dst, window, offsets, lo, hi):
+            nc.vector.tensor_copy(dst, window[:].indirect(offsets[:, lo // 16 : hi // 16]))
+
+        nc.sync.dma_start(list3[:], offs3)
+        fill_scale_rows(day_scales, tab3_scales[0], range(4))
+        nc.sync.dma_start(day_words[:].bitcast(I32), tab3_words[0].bitcast(I32))
+        nc.sync.dma_start(w3_raw_words[:], words_of(w3_words[0]))
+        fill_scale_rows(w3_raw_scales, w3_scales[0], range(4))
+        nc.sync.dma_start(shop_words[0][:].bitcast(I32), words_of(tab_words[0]))
+        nc.sync.dma_start(list1[:], offs)
+        for q in range(4):
+            nc.sync.dma_start(shop_scales[32 * q : 32 * q + 8, :].bitcast(I32), tab_scales[:, 4 * q : 4 * q + 4, :].bitcast(I32))
+        nc.sync.dma_start(shop_words[1][:].bitcast(I32), words_of(tab_words[1]))
+        nc.sync.dma_start(plant_words[:].bitcast(I32), words_of(tab2_words[0]))
+        nc.sync.dma_start(list2[:], offs2)
+        load_scale_rows(plant_scales, tab2_scales[0])
+        w2_rows = w2.rearrange("(p j) c -> p (j c)", j=4)
+        for half in range(2):
+            cols = slice(half * 2 * H, (half + 1) * 2 * H)
+            nc.sync.dma_start(w2_raw[:, cols], w2_rows[:, cols])
+
+        gather(v3_scales[:], day_scales, list3, 0, S)
+        gather(v3_words[0][:], day_words, list3, 0, CHUNK)
+        for g in range(2):
+            reorder(w3_q, w3_raw_words, 8, g, 1)
+            reorder(w3_s, w3_raw_scales, 2, g, 1)
+        v3_words.append(held("w3_raw_scales", S - CHUNK, U16))
+        for lo, hi in ((CHUNK, 2 * CHUNK), (2 * CHUNK, S)):
+            gather(v3_words[1][:, lo - CHUNK : hi - CHUNK], day_words, list3, lo, hi)
+
+        gather(v_scales[0][:], shop_scales, list1, 0, S)
+        for q in range(4):
+            nc.sync.dma_start(v_scales[1][32 * q : 32 * q + 4, :].bitcast(I32), v_scales[0][32 * q + 4 : 32 * q + 8, :].bitcast(I32))
+        nc.sync.dma_start(w1_raw_words[:].rearrange("p (a c) -> p a c", a=2), w1_words.bitcast(I32).rearrange("a p c -> p a c"))
+        for q in range(4):
+            nc.sync.dma_start(
+                w1_raw_scales[32 * q : 32 * q + 4, :].bitcast(I32).rearrange("p (a c) -> p a c", a=2),
+                w1_scales[:, 4 * q : 4 * q + 4, :].bitcast(I32).rearrange("a r c -> r a c"),
+            )
+        w4_rows = w4.rearrange("(q u i) n -> u q i n", u=8, i=8)
+        for u in range(8):
+            g, t = divmod(u, 4)
+            nc.sync.dma_start(w4_raw[g][:, t * N : (t + 1) * N], w4_rows[u])
+
+        for a in range(2):
+            gather(v_words[a][:], shop_words[a], list1, 0, S)
+        gather(v2_words[:], plant_words, list2, 0, S)
+        gather(v2_scales[:], plant_scales, list2, 0, S)
+        for g in range(2):
+            reorder(w1_q, w1_raw_words, 4, g, 2)
+            reorder(w1_s, w1_raw_scales, 2, g, 2)
+
+        def prepare_w2(g):
+            src = w2_raw[:].rearrange("p (j q u h i) -> p u q h j i", j=4, u=8, h=2, i=4)
+            dst = w2_b[g][:].rearrange("p (t q h i j) -> p t q h j i", j=4, t=4, h=2, i=4)
+            for t in range(4):
+                nc.scalar.copy(dst[:, t], src[:, 4 * g + t])
+            nc.vector.quantize_mx(
+                w2_q[:, g * 512 : (g + 1) * 512].bitcast(FP8X4),
+                w2_s[:, g * 512 : (g + 1) * 512],
+                w2_b[g][:],
+            )
+
+        def prepare_w4():
+            w4_b = held("second", 8 * N, BF16)
+            for g in range(2):
+                nc.vector.tensor_copy(
+                    w4_b[:, g * 4 * N : (g + 1) * 4 * N].rearrange("p (c i t) -> p c t i", i=4, t=4),
+                    w4_raw[g][:].rearrange("p (t c i) -> p c t i", i=4, t=4),
+                )
+            nc.vector.quantize_mx(w4_q[:].bitcast(FP8X4), w4_s[:], w4_b[:])
+
+        def unit(k):
+            c, rest = divmod(k, 4)
+            g, jj = divmod(rest, 2)
+            return c, g, jj
+
+        def product(tag, k, passes, first_slot=0):
+            c, g, jj = unit(k)
+            slots = slice(c * CHUNK + jj * P, c * CHUNK + (jj + 1) * P)
+            word_slots = slice(slots.start - first_slot, slots.stop - first_slot)
+            bank = psum.tile([P, 4, P], F32, name=tag, tag=tag)
+            for t in range(4):
+                for a, (wq, ws, base, wtype, vq, vs, vtype) in enumerate(passes):
+                    cols = slice(base + (4 * g + t) * P, base + (4 * g + t + 1) * P)
+                    nc.tensor.matmul_mx(
+                        bank[:, t, :],
+                        lhsT=wq[:, cols].bitcast(wtype), lhsT_scale=ws[:, cols],
+                        rhs=vq[:, word_slots].bitcast(vtype), rhs_scale=vs[:, slots],
+                        start=(a == 0), stop=(a == len(passes) - 1),
+                    )
+            return bank[:].rearrange("p t n -> p n t")
+
+        def woven(tile):
+            return tile.rearrange("p (n t) -> p n t", t=4)
+
+        sines, cosines, mags, h_tiles, reused = {}, {}, {}, {}, []
+
+        def angles(k):
+            part = min(k // 4, 1)
+            d = product("d", k, [(w3_q, w3_s, 0, FP8X4, v3_words[part], v3_scales, FP4X4)], part * CHUNK)
+            if k == EARLY:
+                reused.append(held("w2_raw", 4 * H, F32))
+            if EARLY <= k < EARLY + 3:
+                pair = reused[0][:, (k - EARLY) * 1024 : (k - EARLY + 1) * 1024]
+            elif k % 4 == 1:
+                late_tile = held("late%d" % (k // 4 - 1) if k > 4 else "second", 1024, F32)
+                pair = late_tile[:]
+            else:
+                pair_tile = ring.tile([P, 1024], F32, name="pair", tag="pair", bufs=6)
+                pair = pair_tile[:]
+            sin, cos = pair[:, :512], pair[:, 512:]
+            mag_tile = ring.tile([P, 512], F32, name="mag", tag="mag", bufs=4)
+            mag = mag_tile[:]
+            nc.scalar.activation(woven(sin), d, ACT.Sin)
+            nc.scalar.activation(woven(mag), d, ACT.Abs)
+            nc.scalar.activation(cos, mag, ACT.Sin, bias=math.pi / 2, scale=-1.0)
+            sines[k], cosines[k], mags[k] = sin, cos, mag
+
+        def rotate(k):
+            c, g, jj = unit(k)
+            x = product("x", k, [(w1_q, w1_s, a * H, FP4X4, v_words[a], v_scales[a], FP8X4) for a in range(2)])
+            x_cos = ring.tile([P, 512], F32, name="x_cos", tag="x_cos", bufs=3)
+            nc.vector.tensor_tensor(woven(x_cos[:]), x, woven(cosines[k]), ALU.mult)
+            b = product("b", k, [(w2_q, w2_s, 0, FP8X4, v2_words, v2_scales, FP8X4)])
+            b_sin = ring.tile([P, 512], F32, name="b_sin", tag="b_sin", bufs=4)
+            nc.vector.tensor_tensor(woven(b_sin[:]), b, woven(sines[k]), ALU.mult)
+            if c not in h_tiles:
+                h_tiles[c] = ring.tile([P, 8 * CHUNK], BF16, name="h", tag="h", align_bytes=64)
+            lo = g * 4 * CHUNK + jj * 512
+            engine = nc.vector if k in VECTOR_SUMS else nc.gpsimd
+            engine.tensor_tensor(h_tiles[c][:, lo : lo + 512], x_cos[:], b_sin[:], ALU.add)
+
+        out_rows = out.rearrange("(m p) j -> p m j", p=P)
+
+        banks = {}
+
+        def finish(c):
+            h_q = held("late%d" % c, 2 * CHUNK, U32)
+            h_s = ring.tile([P, 2 * CHUNK], U8, name="h_s", tag="h_s", align_bytes=64)
+            nc.vector.quantize_mx(h_q[:].bitcast(FP8X4), h_s[:], h_tiles[c][:])
+            bank = psum.tile([P, 2, CHUNK], F32, name="y", tag="y")
+            for m in range(2):
+                for g in range(2):
+                    cols = slice(g * N + m * P, g * N + (m + 1) * P)
+                    slots = slice(g * CHUNK, (g + 1) * CHUNK)
+                    nc.tensor.matmul_mx(
+                        bank[:, m, :],
+                        lhsT=w4_q[:, cols].bitcast(FP8X4), lhsT_scale=w4_s[:, cols],
+                        rhs=h_q[:, slots].bitcast(FP8X4), rhs_scale=h_s[:, slots],
+                        start=(g == 0), stop=(g == 1),
+                    )
+            banks[c] = bank
+
+        def store(c):
+            y = mags[STAGE[c]].rearrange("p (m j) -> p m j", m=2)
+            nc.scalar.copy(y, banks[c][:])
+            nc.sync.dma_start(out_rows[:, :, c * CHUNK : (c + 1) * CHUNK], y)
+
+        units = 4 * CHUNKS
+        for k in range(LEAD):
+            angles(k)
+            if k == EARLY - 1:
+                prepare_w2(0)
+                prepare_w2(1)
+        for k in range(units):
+            rotate(k)
+            if k == 1:
+                prepare_w4()
+            if k + LEAD < units:
+                angles(k + LEAD)
+            if k % 4 == 1 and k > 4:
+                finish(k // 4 - 1)
+                store(k // 4 - 1)
+        finish(CHUNKS - 1)
+        store(CHUNKS - 1)

@@ -23,7 +23,7 @@ CHUNKS = S // CHUNK
 LEAD = 8
 EARLY = 6
 STAGE = (11, 15, 14, 13)
-VECTOR_SUMS = (15,)
+VECTOR_SUMS = (3, 7, 11, 15)
 
 
 def tile_list_seasonal_plant_picks_kernel(
@@ -68,7 +68,7 @@ def tile_list_seasonal_plant_picks_kernel(
         w3_s = held("w3_s", H, U8)
         w1_q = held("w1_q", 2 * H, U16)
         w1_s = held("w1_s", 2 * H, U8)
-        w2_b = [held("w2_b%d" % g, 2 * H, BF16) for g in range(2)]
+        w2_b = held("w2_b", 4 * H, BF16)
         w2_q = held("w2_q", H, U32)
         w2_s = held("w2_s", H, U8)
         w4_q = held("w4_q", 2 * N, U32)
@@ -79,9 +79,9 @@ def tile_list_seasonal_plant_picks_kernel(
         nc.vector.memset(plant_scales[:].bitcast(I32), 0)
         nc.gpsimd.memset(w1_raw_scales[:].bitcast(I32), 0)
 
-        def load_scale_rows(tile, rows, quadrants=range(4)):
-            for q in quadrants:
-                nc.sync.dma_start(tile[32 * q : 32 * q + 4, :].bitcast(I32), rows[4 * q : 4 * q + 4, :].bitcast(I32))
+        def load_scale_rows(tile, rows):
+            for r in range(4):
+                nc.sync.dma_start(tile[r:P:32, :].bitcast(I32), rows[r:16:4, :].bitcast(I32))
 
         def fill_scale_rows(tile, rows, quadrants):
             for q in quadrants:
@@ -127,13 +127,13 @@ def tile_list_seasonal_plant_picks_kernel(
             gather(v3_words[1][:, lo - CHUNK : hi - CHUNK], day_words, list3, lo, hi)
 
         gather(v_scales[0][:], shop_scales, list1, 0, S)
-        for q in range(4):
-            nc.sync.dma_start(v_scales[1][32 * q : 32 * q + 4, :].bitcast(I32), v_scales[0][32 * q + 4 : 32 * q + 8, :].bitcast(I32))
+        for r in range(4):
+            nc.sync.dma_start(v_scales[1][r:P:32, :].bitcast(I32), v_scales[0][4 + r : P : 32, :].bitcast(I32))
         nc.sync.dma_start(w1_raw_words[:].rearrange("p (a c) -> p a c", a=2), w1_words.bitcast(I32).rearrange("a p c -> p a c"))
-        for q in range(4):
+        for r in range(4):
             nc.sync.dma_start(
-                w1_raw_scales[32 * q : 32 * q + 4, :].bitcast(I32).rearrange("p (a c) -> p a c", a=2),
-                w1_scales[:, 4 * q : 4 * q + 4, :].bitcast(I32).rearrange("a r c -> r a c"),
+                w1_raw_scales[r:P:32, :].bitcast(I32).rearrange("p (a c) -> p a c", a=2),
+                w1_scales[:, r:16:4, :].bitcast(I32).rearrange("a q c -> q a c"),
             )
         w4_rows = w4.rearrange("(q u i) n -> u q i n", u=8, i=8)
         for u in range(8):
@@ -148,16 +148,12 @@ def tile_list_seasonal_plant_picks_kernel(
             reorder(w1_q, w1_raw_words, 4, g, 2)
             reorder(w1_s, w1_raw_scales, 2, g, 2)
 
-        def prepare_w2(g):
+        def prepare_w2():
             src = w2_raw[:].rearrange("p (j q u h i) -> p u q h j i", j=4, u=8, h=2, i=4)
-            dst = w2_b[g][:].rearrange("p (t q h i j) -> p t q h j i", j=4, t=4, h=2, i=4)
-            for t in range(4):
-                nc.scalar.copy(dst[:, t], src[:, 4 * g + t])
-            nc.vector.quantize_mx(
-                w2_q[:, g * 512 : (g + 1) * 512].bitcast(FP8X4),
-                w2_s[:, g * 512 : (g + 1) * 512],
-                w2_b[g][:],
-            )
+            dst = w2_b[:].rearrange("p (u q h i j) -> p u q h j i", j=4, u=8, h=2, i=4)
+            for u in range(8):
+                nc.scalar.copy(dst[:, u], src[:, u])
+            nc.vector.quantize_mx(w2_q[:].bitcast(FP8X4), w2_s[:], w2_b[:])
 
         def prepare_w4():
             w4_b = held("second", 8 * N, BF16)
@@ -201,11 +197,11 @@ def tile_list_seasonal_plant_picks_kernel(
                 reused.append(held("w2_raw", 4 * H, F32))
             if EARLY <= k < EARLY + 3:
                 pair = reused[0][:, (k - EARLY) * 1024 : (k - EARLY + 1) * 1024]
-            elif k % 4 == 1:
-                late_tile = held("late%d" % (k // 4 - 1) if k > 4 else "second", 1024, F32)
+            elif k == 3:
+                late_tile = held("second", 1024, F32)
                 pair = late_tile[:]
             else:
-                pair_tile = ring.tile([P, 1024], F32, name="pair", tag="pair", bufs=6)
+                pair_tile = ring.tile([P, 1024], F32, name="pair", tag="pair", bufs=8)
                 pair = pair_tile[:]
             sin, cos = pair[:, :512], pair[:, 512:]
             mag_tile = ring.tile([P, 512], F32, name="mag", tag="mag", bufs=4)
@@ -234,7 +230,7 @@ def tile_list_seasonal_plant_picks_kernel(
         banks = {}
 
         def finish(c):
-            h_q = held("late%d" % c, 2 * CHUNK, U32)
+            h_q = ring.tile([P, 2 * CHUNK], U32, name="h_q", tag="h_q", align_bytes=64)
             h_s = ring.tile([P, 2 * CHUNK], U8, name="h_s", tag="h_s", align_bytes=64)
             nc.vector.quantize_mx(h_q[:].bitcast(FP8X4), h_s[:], h_tiles[c][:])
             bank = psum.tile([P, 2, CHUNK], F32, name="y", tag="y")
@@ -259,16 +255,14 @@ def tile_list_seasonal_plant_picks_kernel(
         for k in range(LEAD):
             angles(k)
             if k == EARLY - 1:
-                prepare_w2(0)
-                prepare_w2(1)
+                prepare_w2()
         for k in range(units):
             rotate(k)
-            if k == 1:
+            if k == 3:
                 prepare_w4()
+            if k % 4 == 3:
+                finish(k // 4)
             if k + LEAD < units:
                 angles(k + LEAD)
-            if k % 4 == 1 and k > 4:
-                finish(k // 4 - 1)
-                store(k // 4 - 1)
-        finish(CHUNKS - 1)
-        store(CHUNKS - 1)
+            if k % 4 == 3:
+                store(k // 4)

@@ -23,7 +23,9 @@ CHUNKS = S // CHUNK
 LEAD = 8
 EARLY = 6
 STAGE = (11, 15, 14, 13)
-VECTOR_SUMS = (3, 7, 11, 15)
+TENANT = {5: "late0", 9: "w4_raw0", 10: "w4_raw1", 13: "late2"}
+CODES = ("late0", "w4_raw0", "late2", "late3")
+VECTOR_SUMS = (5, 9, 13, 15)
 
 
 def tile_list_seasonal_plant_picks_kernel(
@@ -61,7 +63,7 @@ def tile_list_seasonal_plant_picks_kernel(
         w3_raw_scales = held("w3_raw_scales", H, U8)
         w1_raw_words = held("w1_raw_words", H, I32)
         w1_raw_scales = held("w1_raw_scales", 2 * H, U8)
-        w2_raw = held("w2_raw", 4 * H, F32)
+        w2_raw = [held("w2_raw%d" % g, 2 * H, F32) for g in range(2)]
         w4_raw = [held("w4_raw%d" % g, 4 * N, F32) for g in range(2)]
 
         w3_q = held("w3_q", H, U32)
@@ -69,53 +71,51 @@ def tile_list_seasonal_plant_picks_kernel(
         w1_q = held("w1_q", 2 * H, U16)
         w1_s = held("w1_s", 2 * H, U8)
         w2_b = held("w2_b", 4 * H, BF16)
-        w2_q = held("w2_q", H, U32)
-        w2_s = held("w2_s", H, U8)
-        w4_q = held("w4_q", 2 * N, U32)
-        w4_s = held("w4_s", 2 * N, U8)
 
+        nc.vector.memset(day_scales[:].bitcast(I32), 0)
+        nc.vector.memset(w3_raw_scales[:].bitcast(I32), 0)
         nc.vector.memset(shop_scales[:].bitcast(I32), 0)
-        nc.gpsimd.memset(v_scales[1][:].bitcast(I32), 0)
         nc.vector.memset(plant_scales[:].bitcast(I32), 0)
-        nc.gpsimd.memset(w1_raw_scales[:].bitcast(I32), 0)
+        nc.vector.memset(v_scales[1][:].bitcast(I32), 0)
+        nc.vector.memset(w1_raw_scales[:].bitcast(I32), 0)
 
-        def load_scale_rows(tile, rows):
-            for r in range(4):
+        def load_scale_rows(tile, rows, which=range(4)):
+            for r in which:
                 nc.sync.dma_start(tile[r:P:32, :].bitcast(I32), rows[r:16:4, :].bitcast(I32))
-
-        def fill_scale_rows(tile, rows, quadrants):
-            for q in quadrants:
-                four = rows[4 * q : 4 * q + 4, :].bitcast(I32)
-                nc.sync.dma_start(tile[32 * q : 32 * q + 32, :].bitcast(I32), four.unsqueeze(0).broadcast_to([8, 4, four.shape[1]]))
 
         def words_of(ap):
             return ap.rearrange("p n t -> p (n t)").bitcast(I32)
 
         def reorder(dst, src, run, g, passes):
             d = dst[:].bitcast(I32).rearrange("p (a g t q i) -> p g a t q i", a=passes, g=2, t=4, i=run)
-            s = src[:].bitcast(I32).rearrange("p (a q g t i) -> p g a t q i", a=passes, g=2, t=4, i=run)
+            s = src[:].bitcast(I32).rearrange("p (a g q t i) -> p g a t q i", a=passes, g=2, t=4, i=run)
             nc.vector.tensor_copy(d[:, g], s[:, g])
 
         def gather(dst, window, offsets, lo, hi):
             nc.vector.tensor_copy(dst, window[:].indirect(offsets[:, lo // 16 : hi // 16]))
 
         nc.sync.dma_start(list3[:], offs3)
-        fill_scale_rows(day_scales, tab3_scales[0], range(4))
+        load_scale_rows(day_scales, tab3_scales[0])
         nc.sync.dma_start(day_words[:].bitcast(I32), tab3_words[0].bitcast(I32))
         nc.sync.dma_start(w3_raw_words[:], words_of(w3_words[0]))
-        fill_scale_rows(w3_raw_scales, w3_scales[0], range(4))
+        load_scale_rows(w3_raw_scales, w3_scales[0])
         nc.sync.dma_start(shop_words[0][:].bitcast(I32), words_of(tab_words[0]))
         nc.sync.dma_start(list1[:], offs)
-        for q in range(4):
-            nc.sync.dma_start(shop_scales[32 * q : 32 * q + 8, :].bitcast(I32), tab_scales[:, 4 * q : 4 * q + 4, :].bitcast(I32))
+        for r in range(4):
+            nc.sync.dma_start(shop_scales[r:P:16, :].bitcast(I32), tab_scales[:, r:16:4, :].bitcast(I32).rearrange("a q c -> q a c"))
         nc.sync.dma_start(shop_words[1][:].bitcast(I32), words_of(tab_words[1]))
         nc.sync.dma_start(plant_words[:].bitcast(I32), words_of(tab2_words[0]))
         nc.sync.dma_start(list2[:], offs2)
-        load_scale_rows(plant_scales, tab2_scales[0])
-        w2_rows = w2.rearrange("(p j) c -> p (j c)", j=4)
-        for half in range(2):
-            cols = slice(half * 2 * H, (half + 1) * 2 * H)
-            nc.sync.dma_start(w2_raw[:, cols], w2_rows[:, cols])
+        load_scale_rows(plant_scales, tab2_scales[0], (0, 1))
+        nc.sync.dma_start(w1_raw_words[:].rearrange("p (a c) -> p a c", a=2), w1_words.bitcast(I32).rearrange("a p c -> p a c"))
+        load_scale_rows(plant_scales, tab2_scales[0], (2, 3))
+        w2_rows = w2.rearrange("(p j) (g c) -> g p j c", j=4, g=2)
+        nc.sync.dma_start(w2_raw[0][:].rearrange("p (j c) -> p j c", j=4), w2_rows[0])
+        for r in range(4):
+            nc.sync.dma_start(
+                w1_raw_scales[r:P:32, :].bitcast(I32).rearrange("p (a c) -> p a c", a=2),
+                w1_scales[:, r:16:4, :].bitcast(I32).rearrange("a q c -> q a c"),
+            )
 
         gather(v3_scales[:], day_scales, list3, 0, S)
         gather(v3_words[0][:], day_words, list3, 0, CHUNK)
@@ -128,17 +128,13 @@ def tile_list_seasonal_plant_picks_kernel(
 
         gather(v_scales[0][:], shop_scales, list1, 0, S)
         for r in range(4):
-            nc.sync.dma_start(v_scales[1][r:P:32, :].bitcast(I32), v_scales[0][4 + r : P : 32, :].bitcast(I32))
-        nc.sync.dma_start(w1_raw_words[:].rearrange("p (a c) -> p a c", a=2), w1_words.bitcast(I32).rearrange("a p c -> p a c"))
-        for r in range(4):
-            nc.sync.dma_start(
-                w1_raw_scales[r:P:32, :].bitcast(I32).rearrange("p (a c) -> p a c", a=2),
-                w1_scales[:, r:16:4, :].bitcast(I32).rearrange("a q c -> q a c"),
-            )
-        w4_rows = w4.rearrange("(q u i) n -> u q i n", u=8, i=8)
-        for u in range(8):
-            g, t = divmod(u, 4)
-            nc.sync.dma_start(w4_raw[g][:, t * N : (t + 1) * N], w4_rows[u])
+            nc.sync.dma_start(v_scales[1][r:P:32, :].bitcast(I32), v_scales[0][16 + r : P : 32, :].bitcast(I32))
+            if r == 1:
+                nc.sync.dma_start(w2_raw[1][:].rearrange("p (j c) -> p j c", j=4), w2_rows[1])
+        w4_rows = w4.rearrange("(g q t i) n -> g t q i n", g=2, t=4, i=8)
+        for g in range(2):
+            for t in range(4):
+                nc.sync.dma_start(w4_raw[g][:, t * N : (t + 1) * N], w4_rows[g, t])
 
         for a in range(2):
             gather(v_words[a][:], shop_words[a], list1, 0, S)
@@ -148,21 +144,23 @@ def tile_list_seasonal_plant_picks_kernel(
             reorder(w1_q, w1_raw_words, 4, g, 2)
             reorder(w1_s, w1_raw_scales, 2, g, 2)
 
+        w2_q = held("w2_q", H, U32)
+        w2_s = held("w2_s", H, U8)
+
         def prepare_w2():
-            src = w2_raw[:].rearrange("p (j q u h i) -> p u q h j i", j=4, u=8, h=2, i=4)
-            dst = w2_b[:].rearrange("p (u q h i j) -> p u q h j i", j=4, u=8, h=2, i=4)
-            for u in range(8):
-                nc.scalar.copy(dst[:, u], src[:, u])
+            dst = w2_b[:].rearrange("p (g t q h i j) -> p g t q h j i", j=4, g=2, t=4, h=2, i=4)
+            for g in range(2):
+                src = w2_raw[g][:].rearrange("p (j q t h i) -> p t q h j i", j=4, t=4, h=2, i=4)
+                for t in range(4):
+                    nc.scalar.copy(dst[:, g, t], src[:, t])
             nc.vector.quantize_mx(w2_q[:].bitcast(FP8X4), w2_s[:], w2_b[:])
 
-        def prepare_w4():
-            w4_b = held("second", 8 * N, BF16)
+        def round_w4():
             for g in range(2):
-                nc.vector.tensor_copy(
-                    w4_b[:, g * 4 * N : (g + 1) * 4 * N].rearrange("p (c i t) -> p c t i", i=4, t=4),
+                nc.scalar.copy(
+                    h_tiles[0][:, g * 4 * N : (g + 1) * 4 * N].rearrange("p (c i t) -> p c t i", i=4, t=4),
                     w4_raw[g][:].rearrange("p (t c i) -> p c t i", i=4, t=4),
                 )
-            nc.vector.quantize_mx(w4_q[:].bitcast(FP8X4), w4_s[:], w4_b[:])
 
         def unit(k):
             c, rest = divmod(k, 4)
@@ -188,20 +186,20 @@ def tile_list_seasonal_plant_picks_kernel(
         def woven(tile):
             return tile.rearrange("p (n t) -> p n t", t=4)
 
-        sines, cosines, mags, h_tiles, reused = {}, {}, {}, {}, []
+        sines, cosines, mags, h_tiles, parts, w4_mx, reused = {}, {}, {}, {}, {}, [], []
 
         def angles(k):
             part = min(k // 4, 1)
             d = product("d", k, [(w3_q, w3_s, 0, FP8X4, v3_words[part], v3_scales, FP4X4)], part * CHUNK)
             if k == EARLY:
-                reused.append(held("w2_raw", 4 * H, F32))
-            if EARLY <= k < EARLY + 3:
+                reused.append(held("w2_raw1", 2048, F32))
+            if k in (EARLY, EARLY + 1):
                 pair = reused[0][:, (k - EARLY) * 1024 : (k - EARLY + 1) * 1024]
-            elif k == 3:
-                late_tile = held("second", 1024, F32)
-                pair = late_tile[:]
+            elif k in TENANT:
+                pair_tile = held(TENANT[k], 1024, F32)
+                pair = pair_tile[:]
             else:
-                pair_tile = ring.tile([P, 1024], F32, name="pair", tag="pair", bufs=8)
+                pair_tile = ring.tile([P, 1024], F32, name="pair", tag="pair", bufs=7)
                 pair = pair_tile[:]
             sin, cos = pair[:, :512], pair[:, 512:]
             mag_tile = ring.tile([P, 512], F32, name="mag", tag="mag", bufs=4)
@@ -219,37 +217,58 @@ def tile_list_seasonal_plant_picks_kernel(
             b = product("b", k, [(w2_q, w2_s, 0, FP8X4, v2_words, v2_scales, FP8X4)])
             b_sin = ring.tile([P, 512], F32, name="b_sin", tag="b_sin", bufs=4)
             nc.vector.tensor_tensor(woven(b_sin[:]), b, woven(sines[k]), ALU.mult)
+            parts[k] = (x_cos, b_sin)
+
+        def add_parts(k):
+            c, g, jj = unit(k)
+            lead = 8 * N if c == 0 else 0
             if c not in h_tiles:
-                h_tiles[c] = ring.tile([P, 8 * CHUNK], BF16, name="h", tag="h", align_bytes=64)
-            lo = g * 4 * CHUNK + jj * 512
+                h_tiles[c] = held("h", lead + 8 * CHUNK, BF16)
+            lo = lead + g * 4 * CHUNK + jj * 512
             engine = nc.vector if k in VECTOR_SUMS else nc.gpsimd
-            engine.tensor_tensor(h_tiles[c][:, lo : lo + 512], x_cos[:], b_sin[:], ALU.add)
+            engine.tensor_tensor(h_tiles[c][:, lo : lo + 512], parts[k][0][:], parts[k][1][:], ALU.add)
 
         out_rows = out.rearrange("(m p) j -> p m j", p=P)
 
         banks = {}
 
         def finish(c):
-            h_q = ring.tile([P, 2 * CHUNK], U32, name="h_q", tag="h_q", align_bytes=64)
-            h_s = ring.tile([P, 2 * CHUNK], U8, name="h_s", tag="h_s", align_bytes=64)
-            nc.vector.quantize_mx(h_q[:].bitcast(FP8X4), h_s[:], h_tiles[c][:])
-            bank = psum.tile([P, 2, CHUNK], F32, name="y", tag="y")
+            lead = 2 * N if c == 0 else 0
+            codes = held(CODES[c], lead + 2 * CHUNK, U32)
+            scales = held("h_s%d" % c, lead + 2 * CHUNK, U8)
+            nc.vector.quantize_mx(codes[:].bitcast(FP8X4), scales[:], h_tiles[c][:])
+            if c == 0:
+                w4_mx.extend([codes, scales])
+            w4_q, w4_s = w4_mx
+            h_q, h_s = codes, scales
+            last = c == CHUNKS - 1
+            halves = []
             for m in range(2):
+                if m == 0 or last:
+                    bank = psum.tile([P, 2, CHUNK], F32, name="y", tag="y")
+                halves.append(bank)
                 for g in range(2):
                     cols = slice(g * N + m * P, g * N + (m + 1) * P)
-                    slots = slice(g * CHUNK, (g + 1) * CHUNK)
+                    slots = slice(lead + g * CHUNK, lead + (g + 1) * CHUNK)
                     nc.tensor.matmul_mx(
                         bank[:, m, :],
                         lhsT=w4_q[:, cols].bitcast(FP8X4), lhsT_scale=w4_s[:, cols],
                         rhs=h_q[:, slots].bitcast(FP8X4), rhs_scale=h_s[:, slots],
                         start=(g == 0), stop=(g == 1),
                     )
-            banks[c] = bank
+            banks[c] = halves
 
         def store(c):
             y = mags[STAGE[c]].rearrange("p (m j) -> p m j", m=2)
-            nc.scalar.copy(y, banks[c][:])
-            nc.sync.dma_start(out_rows[:, :, c * CHUNK : (c + 1) * CHUNK], y)
+            rows = out_rows[:, :, c * CHUNK : (c + 1) * CHUNK]
+            if c < CHUNKS - 1:
+                nc.scalar.copy(y, banks[c][0][:])
+                nc.sync.dma_start(rows, y)
+            else:
+                nc.scalar.copy(y[:, 0, :], banks[c][0][:, 0, :])
+                nc.scalar.dma_start(rows[:, 0, :], y[:, 0, :])
+                nc.vector.tensor_copy(y[:, 1, :], banks[c][1][:, 1, :])
+                nc.sync.dma_start(rows[:, 1, :], y[:, 1, :])
 
         units = 4 * CHUNKS
         for k in range(LEAD):
@@ -258,11 +277,17 @@ def tile_list_seasonal_plant_picks_kernel(
                 prepare_w2()
         for k in range(units):
             rotate(k)
-            if k == 3:
-                prepare_w4()
-            if k % 4 == 3:
-                finish(k // 4)
+            if k % 4 == 1 and k > 4:
+                finish(k // 4 - 1)
+                add_parts(k)
+                add_parts(k - 1)
+            elif k % 4 != 0 or k == 0:
+                add_parts(k)
             if k + LEAD < units:
                 angles(k + LEAD)
-            if k % 4 == 3:
-                store(k // 4)
+            if k == 0:
+                round_w4()
+            if k % 4 == 1 and k > 4:
+                store(k // 4 - 1)
+        finish(CHUNKS - 1)
+        store(CHUNKS - 1)

import math
from contextlib import ExitStack

import concourse.mybir as mybir

K, K2, H, N, T, S = 1024, 512, 1024, 256, 2048, 1024
FLOPS = 2 * S * (K * H + 2 * K2 * H + H * N)

F32 = mybir.dt.float32
BF16 = mybir.dt.bfloat16
I32 = mybir.dt.int32
U32 = mybir.dt.uint32
U16 = mybir.dt.uint16
U8 = mybir.dt.uint8
FP8X4 = mybir.dt.float8_e4m3fn_x4
FP4X4 = mybir.dt.float4_e2m1fn_x4
ACT = mybir.ActivationFunctionType
ALU = mybir.AluOpType

P = 128
CHUNK = 256
CHUNKS = S // CHUNK
LEAD = 8
EARLY = 6
STAGE = (11, 15, 14, 13)
TENANT = {5: "late0", 9: "w4_raw0", 10: "w4_raw1", 13: "late2"}
CODES = ("late0", "w4_raw0", "late2", "late3")
VECTOR_SUMS = (5, 9, 13, 15)


def tile_list_seasonal_plant_picks_kernel(
    tc, tab_words, tab_scales, tab2_words, tab2_scales, tab3_words, tab3_scales,
    offs, offs2, offs3, w1_words, w1_scales, w2, w3_words, w3_scales, w4, out,
):
    nc = tc.nc
    with ExitStack() as ctx:
        keep = ctx.enter_context(tc.tile_pool(name="keep", bufs=1))
        ring = ctx.enter_context(tc.tile_pool(name="ring", bufs=2))
        psum = ctx.enter_context(tc.psum_pool(name="psum", bufs=2))

        def held(name, columns, dtype):
            return keep.tile([P, columns], dtype, name=name, align_bytes=64)

        list1 = keep.tile([P, S // 16], U16, name="list1")
        list2 = keep.tile([P, S // 16], U16, name="list2")
        list3 = keep.tile([P, S // 16], U16, name="list3")

        day_words = held("day_words", T, U16)
        day_scales = held("day_scales", T, U8)
        shop_words = [held("shop_words%d" % a, T, U32) for a in range(2)]
        shop_scales = held("shop_scales", T, U8)
        plant_words = held("plant_words", T, U32)
        plant_scales = held("plant_scales", T, U8)

        v3_words = [held("v3_words", CHUNK, U16)]
        v3_scales = held("v3_scales", S, U8)
        v_words = [held("v_words%d" % a, S, U32) for a in range(2)]
        v_scales = [held("v_scales%d" % a, S, U8) for a in range(2)]
        v2_words = held("v2_words", S, U32)
        v2_scales = held("v2_scales", S, U8)

        w3_raw_words = held("w3_raw_words", H, I32)
        w3_raw_scales = held("w3_raw_scales", H, U8)
        w1_raw_words = held("w1_raw_words", H, I32)
        w1_raw_scales = held("w1_raw_scales", 2 * H, U8)
        w2_raw = [held("w2_raw%d" % g, 2 * H, F32) for g in range(2)]
        w4_raw = [held("w4_raw%d" % g, 4 * N, F32) for g in range(2)]

        w3_q = held("w3_q", H, U32)
        w3_s = held("w3_s", H, U8)
        w1_q = held("w1_q", 2 * H, U16)
        w1_s = held("w1_s", 2 * H, U8)
        w2_b = held("w2_b", 4 * H, BF16)

        nc.vector.memset(day_scales[:].bitcast(I32), 0)
        nc.vector.memset(w3_raw_scales[:].bitcast(I32), 0)
        nc.vector.memset(shop_scales[:].bitcast(I32), 0)
        nc.vector.memset(plant_scales[:].bitcast(I32), 0)
        nc.vector.memset(v_scales[1][:].bitcast(I32), 0)
        nc.vector.memset(w1_raw_scales[:].bitcast(I32), 0)

        def load_scale_rows(tile, rows, which=range(4)):
            for r in which:
                nc.sync.dma_start(tile[r:P:32, :].bitcast(I32), rows[r:16:4, :].bitcast(I32))

        def words_of(ap):
            return ap.rearrange("p n t -> p (n t)").bitcast(I32)

        def reorder(dst, src, run, g, passes):
            d = dst[:].bitcast(I32).rearrange("p (a g t q i) -> p g a t q i", a=passes, g=2, t=4, i=run)
            s = src[:].bitcast(I32).rearrange("p (a g q t i) -> p g a t q i", a=passes, g=2, t=4, i=run)
            nc.vector.tensor_copy(d[:, g], s[:, g])

        def gather(dst, window, offsets, lo, hi):
            nc.vector.tensor_copy(dst, window[:].indirect(offsets[:, lo // 16 : hi // 16]))

        nc.sync.dma_start(list3[:], offs3)
        load_scale_rows(day_scales, tab3_scales[0])
        nc.sync.dma_start(day_words[:].bitcast(I32), tab3_words[0].bitcast(I32))
        nc.sync.dma_start(w3_raw_words[:], words_of(w3_words[0]))
        load_scale_rows(w3_raw_scales, w3_scales[0])
        nc.sync.dma_start(shop_words[0][:].bitcast(I32), words_of(tab_words[0]))
        nc.sync.dma_start(list1[:], offs)
        for r in range(4):
            nc.sync.dma_start(shop_scales[r:P:16, :].bitcast(I32), tab_scales[:, r:16:4, :].bitcast(I32).rearrange("a q c -> q a c"))
        nc.sync.dma_start(shop_words[1][:].bitcast(I32), words_of(tab_words[1]))
        nc.sync.dma_start(plant_words[:].bitcast(I32), words_of(tab2_words[0]))
        nc.sync.dma_start(list2[:], offs2)
        load_scale_rows(plant_scales, tab2_scales[0], (0, 1))
        nc.sync.dma_start(w1_raw_words[:].rearrange("p (a c) -> p a c", a=2), w1_words.bitcast(I32).rearrange("a p c -> p a c"))
        load_scale_rows(plant_scales, tab2_scales[0], (2, 3))
        w2_rows = w2.rearrange("(p j) (g c) -> g p j c", j=4, g=2)
        nc.sync.dma_start(w2_raw[0][:].rearrange("p (j c) -> p j c", j=4), w2_rows[0])
        for r in range(4):
            nc.sync.dma_start(
                w1_raw_scales[r:P:32, :].bitcast(I32).rearrange("p (a c) -> p a c", a=2),
                w1_scales[:, r:16:4, :].bitcast(I32).rearrange("a q c -> q a c"),
            )

        gather(v3_scales[:], day_scales, list3, 0, S)
        gather(v3_words[0][:], day_words, list3, 0, CHUNK)
        for g in range(2):
            reorder(w3_q, w3_raw_words, 8, g, 1)
            reorder(w3_s, w3_raw_scales, 2, g, 1)
        v3_words.append(held("w3_raw_scales", S - CHUNK, U16))
        for lo, hi in ((CHUNK, 2 * CHUNK), (2 * CHUNK, S)):
            gather(v3_words[1][:, lo - CHUNK : hi - CHUNK], day_words, list3, lo, hi)

        gather(v_scales[0][:], shop_scales, list1, 0, S)
        for r in range(4):
            nc.sync.dma_start(v_scales[1][r:P:32, :].bitcast(I32), v_scales[0][16 + r : P : 32, :].bitcast(I32))
            if r == 1:
                nc.sync.dma_start(w2_raw[1][:].rearrange("p (j c) -> p j c", j=4), w2_rows[1])
        w4_rows = w4.rearrange("(g q t i) n -> g t q i n", g=2, t=4, i=8)
        for g in range(2):
            for t in range(4):
                nc.sync.dma_start(w4_raw[g][:, t * N : (t + 1) * N], w4_rows[g, t])

        for a in range(2):
            gather(v_words[a][:], shop_words[a], list1, 0, S)
        gather(v2_words[:], plant_words, list2, 0, S)
        gather(v2_scales[:], plant_scales, list2, 0, S)
        for g in range(2):
            reorder(w1_q, w1_raw_words, 4, g, 2)
            reorder(w1_s, w1_raw_scales, 2, g, 2)

        w2_q = held("w2_q", H, U32)
        w2_s = held("w2_s", H, U8)

        def prepare_w2():
            dst = w2_b[:].rearrange("p (g t q h i j) -> p g t q h j i", j=4, g=2, t=4, h=2, i=4)
            for g in range(2):
                src = w2_raw[g][:].rearrange("p (j q t h i) -> p t q h j i", j=4, t=4, h=2, i=4)
                for t in range(4):
                    nc.scalar.copy(dst[:, g, t], src[:, t])
            nc.vector.quantize_mx(w2_q[:].bitcast(FP8X4), w2_s[:], w2_b[:])

        def round_w4():
            for g in range(2):
                nc.scalar.copy(
                    h_tiles[0][:, g * 4 * N : (g + 1) * 4 * N].rearrange("p (c i t) -> p c t i", i=4, t=4),
                    w4_raw[g][:].rearrange("p (t c i) -> p c t i", i=4, t=4),
                )

        def unit(k):
            c, rest = divmod(k, 4)
            g, jj = divmod(rest, 2)
            return c, g, jj

        def product(tag, k, passes, first_slot=0):
            c, g, jj = unit(k)
            slots = slice(c * CHUNK + jj * P, c * CHUNK + (jj + 1) * P)
            word_slots = slice(slots.start - first_slot, slots.stop - first_slot)
            bank = psum.tile([P, 4, P], F32, name=tag, tag=tag)
            for t in range(4):
                for a, (wq, ws, base, wtype, vq, vs, vtype) in enumerate(passes):
                    cols = slice(base + (4 * g + t) * P, base + (4 * g + t + 1) * P)
                    nc.tensor.matmul_mx(
                        bank[:, t, :],
                        lhsT=wq[:, cols].bitcast(wtype), lhsT_scale=ws[:, cols],
                        rhs=vq[:, word_slots].bitcast(vtype), rhs_scale=vs[:, slots],
                        start=(a == 0), stop=(a == len(passes) - 1),
                    )
            return bank[:].rearrange("p t n -> p n t")

        def woven(tile):
            return tile.rearrange("p (n t) -> p n t", t=4)

        sines, cosines, mags, h_tiles, parts, w4_mx, reused = {}, {}, {}, {}, {}, [], []

        def angles(k):
            part = min(k // 4, 1)
            d = product("d", k, [(w3_q, w3_s, 0, FP8X4, v3_words[part], v3_scales, FP4X4)], part * CHUNK)
            if k == EARLY:
                reused.append(held("w2_raw1", 2048, F32))
            if k in (EARLY, EARLY + 1):
                pair = reused[0][:, (k - EARLY) * 1024 : (k - EARLY + 1) * 1024]
            elif k in TENANT:
                pair_tile = held(TENANT[k], 1024, F32)
                pair = pair_tile[:]
            else:
                pair_tile = ring.tile([P, 1024], F32, name="pair", tag="pair", bufs=7)
                pair = pair_tile[:]
            sin, cos = pair[:, :512], pair[:, 512:]
            mag_tile = ring.tile([P, 512], F32, name="mag", tag="mag", bufs=4)
            mag = mag_tile[:]
            nc.scalar.activation(woven(sin), d, ACT.Sin)
            nc.scalar.activation(woven(mag), d, ACT.Abs)
            nc.scalar.activation(cos, mag, ACT.Sin, bias=math.pi / 2, scale=-1.0)
            sines[k], cosines[k], mags[k] = sin, cos, mag

        def rotate(k):
            c, g, jj = unit(k)
            x = product("x", k, [(w1_q, w1_s, a * H, FP4X4, v_words[a], v_scales[a], FP8X4) for a in range(2)])
            x_cos = ring.tile([P, 512], F32, name="x_cos", tag="x_cos", bufs=3)
            nc.vector.tensor_tensor(woven(x_cos[:]), x, woven(cosines[k]), ALU.mult)
            b = product("b", k, [(w2_q, w2_s, 0, FP8X4, v2_words, v2_scales, FP8X4)])
            b_sin = ring.tile([P, 512], F32, name="b_sin", tag="b_sin", bufs=4)
            nc.vector.tensor_tensor(woven(b_sin[:]), b, woven(sines[k]), ALU.mult)
            parts[k] = (x_cos, b_sin)

        def add_parts(k):
            c, g, jj = unit(k)
            lead = 8 * N if c == 0 else 0
            if c not in h_tiles:
                h_tiles[c] = held("h", lead + 8 * CHUNK, BF16)
            lo = lead + g * 4 * CHUNK + jj * 512
            engine = nc.vector if k in VECTOR_SUMS else nc.gpsimd
            engine.tensor_tensor(h_tiles[c][:, lo : lo + 512], parts[k][0][:], parts[k][1][:], ALU.add)

        out_rows = out.rearrange("(m p) j -> p m j", p=P)

        banks = {}

        def finish(c):
            lead = 2 * N if c == 0 else 0
            codes = held(CODES[c], lead + 2 * CHUNK, U32)
            scales = held("h_s%d" % c, lead + 2 * CHUNK, U8)
            nc.vector.quantize_mx(codes[:].bitcast(FP8X4), scales[:], h_tiles[c][:])
            if c == 0:
                w4_mx.extend([codes, scales])
            w4_q, w4_s = w4_mx
            h_q, h_s = codes, scales
            last = c == CHUNKS - 1
            halves = []
            for m in range(2):
                if m == 0 or last:
                    bank = psum.tile([P, 2, CHUNK], F32, name="y", tag="y")
                halves.append(bank)
                for g in range(2):
                    cols = slice(g * N + m * P, g * N + (m + 1) * P)
                    slots = slice(lead + g * CHUNK, lead + (g + 1) * CHUNK)
                    nc.tensor.matmul_mx(
                        bank[:, m, :],
                        lhsT=w4_q[:, cols].bitcast(FP8X4), lhsT_scale=w4_s[:, cols],
                        rhs=h_q[:, slots].bitcast(FP8X4), rhs_scale=h_s[:, slots],
                        start=(g == 0), stop=(g == 1),
                    )
            banks[c] = halves

        def store(c):
            y = mags[STAGE[c]].rearrange("p (m j) -> p m j", m=2)
            rows = out_rows[:, :, c * CHUNK : (c + 1) * CHUNK]
            if c < CHUNKS - 1:
                nc.scalar.copy(y, banks[c][0][:])
                nc.sync.dma_start(rows, y)
            else:
                nc.scalar.copy(y[:, 0, :], banks[c][0][:, 0, :])
                nc.scalar.dma_start(rows[:, 0, :], y[:, 0, :])
                nc.vector.tensor_copy(y[:, 1, :], banks[c][1][:, 1, :])
                nc.sync.dma_start(rows[:, 1, :], y[:, 1, :])

        units = 4 * CHUNKS
        for k in range(LEAD):
            angles(k)
            if k == EARLY - 1:
                prepare_w2()
        for k in range(units):
            rotate(k)
            if k % 4 == 1 and k > 4:
                finish(k // 4 - 1)
                add_parts(k)
                add_parts(k - 1)
            elif k % 4 != 0 or k == 0:
                add_parts(k)
            if k + LEAD < units:
                angles(k + LEAD)
            if k == 0:
                round_w4()
            if k % 4 == 1 and k > 4:
                store(k // 4 - 1)
        finish(CHUNKS - 1)
        store(CHUNKS - 1)
